import numpy as np, ml_dtypes
CORES = [16,17,18,19,32,33,34,35]
N = 8
BF = ml_dtypes.bfloat16
def gentries(a):
    return np.ascontiguousarray(a.reshape(8, 16, -1).transpose(0, 2, 1)).reshape(8, -1)
def gtable(e):
    e = np.asarray(e); return np.ascontiguousarray(e.reshape(8, -1, 16).transpose(0, 2, 1)).reshape(128, -1).astype(np.int32)
V, R, K, S, RO = 4096, 4096, 2048, 4, 2
def take(a, j):
    return np.take_along_axis(a, j, 2)
def parts(rng, x):
    rec = rng.integers(0, R, (N, 8, V)); pri = take(np.sum(x, axis=2), rec); m = V - 1; q = np.arange(m)
    o = 1 + np.argsort(-pri[..., 1:], axis=2, kind="stable"); ch = []
    for side in range(2):
        u = rng.random((N, 8, m)); p = np.minimum(q + 1 + ((m - 1 - q) * u * u * u).astype(np.int64), m - 1)
        k = np.where((rng.random((N, 8, m)) < 0.1) | (q == m - 1), 0, take(o, p))
        a = rng.integers(0, V, (N, 8, V)); np.put_along_axis(a, o, k, 2); ch.append(a)
    u = rng.random((N, 8, K)); rt = np.where(rng.random((N, 8, K)) < 0.03, 0, take(o, (m * u * u).astype(np.int64)))
    return rec, ch[0], ch[1], rt, rng.integers(0, 256, (N, 8, 16))
def people(rng):
    big = rng.random((N, 8, 16, K)) < 0.35
    return np.where(rng.random((N, 8, 1, K)) < 0.5, rng.integers(0, 16, big.shape), np.where(big, rng.integers(12, 16, big.shape), rng.integers(0, 7, big.shape)))
def pack(x, y, rec, lc, rc, rt, w):
    return {"x": np.ascontiguousarray(x).reshape(N, 128, R).astype(BF), "nw": np.ascontiguousarray(y).reshape(N, 128, K).astype(BF),
            "rec": rec.astype(np.int32), "lc": lc.astype(np.int32), "rc": rc.astype(np.int32), "rt": np.stack([gtable(a) for a in rt]),
            "wt": np.ascontiguousarray(w).reshape(N, 128, 1).astype(np.int32)}
def setup_inputs(rng):
    x = rng.integers(0, 16, (N, 8, 16, R))
    return pack(x, people(rng), *parts(rng, x))
def setup_inputs_ties(rng):
    c = [[8] * 8 + [7, 7, 6, 6, 6, 6, 5, 5], [8] * 8 + [7, 7, 6, 6, 6, 5, 5, 5], [9] + [8] * 7 + [7, 7, 6, 6, 6, 6, 5, 5],
         [8] * 9 + [6, 6, 6, 6, 6, 5, 5], [8] * 9 + [6, 6, 6, 6, 5, 5, 5], [9] + [8] * 8 + [6, 6, 6, 6, 6, 5, 5]]
    a = np.array(c)[rng.integers(0, 6, (N, 8, R))]
    x = np.take_along_axis(a, np.argsort(rng.random(a.shape), axis=3), 3).transpose(0, 1, 3, 2)
    u = rng.random((N, 8, 1, R)); x = np.where(u < 0.06, 0, np.where(u > 0.94, np.where(rng.random(x.shape) < 0.2, 14, 15), x))
    rec, lc, rc, rt, w = parts(rng, x)
    lc = rng.integers(0, V, lc.shape); rc = rng.integers(0, V, rc.shape)
    u = rng.random((N, 8, 1, K)); y = np.where(u < 0.6, 7, people(rng))
    return pack(x, np.where(u > 0.9, np.where(rng.random(y.shape) < 0.15, 14, 15), y), rec, lc, rc, rt, w)
def setup_inputs_ends(rng):
    x = rng.integers(0, 16, (N, 8, 16, R)); rec, lc, rc, rt, w = parts(rng, x)
    lc = np.where(rng.random(lc.shape) < 0.4, 0, lc); rc = np.where(rng.random(rc.shape) < 0.4, 0, rc)
    e = np.array([0, 1, V - 1])
    lc[:, 1] = rng.choice(e, (N, V)); rc[:, 1] = rng.choice(e, (N, V)); rt[:, 1] = rng.choice(e, (N, K))
    rec[:, 2] = rng.choice(np.array([0, R - 1]), (N, V)); rt[:, 3] = rng.choice(e, (N, K))
    rec[:, 4:, 1] = R - 1; rec[:, 4:, V - 1] = 0; rt[:, 5, 0] = V - 1; rt[:, 5, K - 1] = 1
    for q in range(N): rt[q, (q + int(rng.integers(0, 2))) % 8] = 0
    return pack(x, people(rng), rec, lc, rc, rt, w)
def setup_inputs_long(rng):
    x = rng.integers(0, 16, (N, 8, 16, R)); y = people(rng); half = R // 2
    x[:, 0] = rng.integers(1, 16, (N, 16, R)); y[:, 0] = 0
    y[:, 1] = 15; x[:, 1, :, ::16] = 15
    x[:, 2] = rng.integers(9, 16, (N, 16, R)); y[:, 2, :9] = 15; y[:, 2, 9:] = 0
    x[:, 3, 7:] = rng.integers(1, 4, (N, 9, R)); y[:, 3, 7:] = 0; y[:, 3, :7] = 15
    for g in range(4, 8):
        x[:, g, :, :half] = rng.integers(9, 16, (N, 16, half)); x[:, g, :, half:] = rng.integers(0, 7, (N, 16, R - half))
        y[:, g] = np.where(rng.random((N, 1, K)) < 0.5, rng.integers(7, 9, (N, 16, K)), np.where(np.arange(16)[:, None] < 9, 15, 0))
    rec, lc, rc, rt, w = parts(rng, x); out = []
    for a in (lc, rc, rt): out.append(np.where(a == 0, rng.integers(1, V, a.shape), a))
    for g in range(4, 8):
        h = min(g - 3, S - 1); m = V // (h + 1); lev = np.arange(V) % (h + 1)
        for k in range(2): out[k][:, g] = np.where(lev < h, (h + 1) * rng.integers(0, m, (N, V)) + lev + 1, out[k][:, g])
        out[2][:, g] = (h + 1) * rng.integers(1, m, (N, K))
        rec[:, g] = rng.integers(0, half, (N, V)) + np.where(lev == h, half, 0)
    return pack(x, y, rec, out[0], out[1], out[2], w)
def setup_inputs_alike(rng):
    x = rng.integers(0, 16, (N, 8, 16, R)); rec, lc, rc, rt, w = parts(rng, x); y = people(rng); v = np.arange(V)
    rt[:, 0] = rng.integers(1, V, (N, 1)); rt[:, 2] = rng.choice(np.array([1, V - 1, 5]), (N, K))
    rec[:, 1] = rng.integers(0, R, (N, 1)); rec[:, 3] = rng.choice(np.array([0, R - 1, 17]), (N, V))
    lc[:, 4] = np.where(rng.random((N, V)) < 0.5, v, lc[:, 4]); rc[:, 5] = np.where(rng.random((N, V)) < 0.5, v, rc[:, 5]); rc[:, 6] = lc[:, 6]
    y[:, 7] = y[:, 7, :, :1]; y[:, 2, :, ::2] = y[:, 2, :, :1]
    w[0] = 0; w[1] = 255; w[2:] = 0; w[2:, :, int(rng.integers(0, 16))] = rng.integers(1, 256, (N - 2, 8))
    q = K // 4; rt[0, 3, :q] = 0
    y[0, 3, :, :q] = np.where((rng.random((16, q)) < 0.25) & (np.arange(q) % 2 == 1), 14, 15)
    return pack(x, y, rec, lc, rc, rt, w)
def setup_inputs_spread(rng):
    x = (16 * rng.random((N, 8, 16, R)) ** np.exp2(rng.integers(-2, 3, (N, 8, 1, R)))).astype(np.int64)
    y = (16 * rng.random((N, 8, 16, K)) ** np.exp2(rng.integers(-2, 3, (N, 8, 1, K)))).astype(np.int64)
    rec, lc, rc, rt, w = parts(rng, np.minimum(x, 15))
    return pack(np.minimum(x, 15), np.minimum(y, 15), rec, lc, rc, rt, np.minimum((256 * rng.random((N, 8, 16)) ** 4).astype(np.int64), 255))
def check_inputs(d):
    bad = []
    for k in ("x", "nw"):
        a = np.asarray(d[k]).astype(np.float32)
        if not bool(np.all((a >= 0) & (a <= 15) & (a == np.floor(a)))): bad.append("whole numbers and range of " + k)
    for k, hi in (("rec", R - 1), ("lc", V - 1), ("rc", V - 1), ("rt", V - 1), ("wt", 255)):
        if np.min(d[k]) < 0 or np.max(d[k]) > hi: bad.append("range of " + k)
    return bad
def reference(x, nw, rec, lc, rc, rt, wt):
    nodes = V + RO * (S + 1) * K; lane = np.zeros((N, 8, K), np.int64) + np.arange(K)
    xs = np.zeros((N, 8, 16, R + RO * K), np.int64); xs[..., :R] = x.astype(np.float32).astype(np.int64).reshape(N, 8, 16, R)
    y = nw.astype(np.float32).astype(np.int64).reshape(N, 8, 16, K); w = wt.astype(np.int64).reshape(N, 8, 16, 1)
    of = np.zeros((N, 8, nodes), np.int64); of[..., :V] = rec
    pt = np.zeros((N, 8, 2 * nodes + 2 * K), np.int64); pt[..., 0:2 * V:2] = lc; pt[..., 1:2 * V:2] = rc
    def put(m, at, v):
        np.put_along_axis(pt, np.where(m, at, 2 * nodes + K + lane), v, 2)
    c = np.stack([gentries(a) for a in rt]).astype(np.int64)
    for t in range(RO):
        b = V + t * (S + 1) * K; new = b + S * K + lane
        xs[..., R + t * K:R + (t + 1) * K] = y; of[..., b + S * K:b + (S + 1) * K] = R + t * K + lane
        py = np.sum(y, axis=2); hung = lane < 0; went = lane < 0; last = lane * 0
        hole = 2 * nodes + lane; lh = lane * 0; rh = lane * 0; opened = lane * 0
        for s in range(S):
            live = c > 0; n = b + s * K + lane; rn = take(of, c); xc = np.take_along_axis(xs, rn[:, :, None, :], 3)
            hang = live & ~hung & (np.sum(xc, axis=2) < py)
            put(hang, hole, new); lh = np.where(hang, 2 * new, lh); rh = np.where(hang, 2 * new + 1, rh); hung = hung | hang
            high = np.sum(xc > y, axis=2) >= 9
            l = take(pt, 2 * c); r = take(pt, 2 * c + 1)
            of[..., b + s * K:b + (s + 1) * K] = np.where(live, rn, 0); put(live, 2 * n, l); put(live, 2 * n + 1, r)
            put(live, np.where(hung, np.where(high, rh, lh), hole), n)
            opened = np.where(live, np.where(high, 2 * n, 2 * n + 1), opened)
            hole = np.where(live & ~hung, opened, hole)
            lh = np.where(live & hung & ~high, opened, lh); rh = np.where(live & hung & high, opened, rh)
            last = np.where(live, rn, last); went = went | live
            c = np.where(live, np.where(high, l, r), 0)
        xc = np.take_along_axis(xs, take(of, c)[:, :, None, :], 3); high = np.sum(xc > y, axis=2) >= 9
        put(~hung, hole, new); put(~hung & (c > 0), np.where(high, 2 * new + 1, 2 * new), c)
        put(hung, lh, 0); put(hung, rh, 0); put(hung, opened, c)
        made = np.array(pt[..., 2 * nodes:2 * nodes + K])
        if t < RO - 1:
            xl = np.where(went[:, :, None, :], np.take_along_axis(xs, last[:, :, None, :], 3), 0)
            y = np.roll((y + xl + t) & 15, 1, axis=0)
            c = take(made, np.sum(w * y, axis=2) & (K - 1))
    return {"yl": pt[..., 2 * V:2 * nodes:2].astype(np.float32), "yr": pt[..., 2 * V + 1:2 * nodes:2].astype(np.float32), "yt": made.astype(np.float32)}

import numpy as np
from concourse.bass import DstId, RemoteDMATransfer
from concourse.mybir import AluOpType, ActivationFunctionType

F32, BF, I32, U16 = "float32", "bfloat16", "int32", "uint16"
SB = {
    BF: {"xs": [4096], "X": [6144], "tab": [14336], "yp": [2048], "y1": [2048], "gi": [2048], "gx": [2048], "vv": [2048], "tn": [2048],
         "hi0": [768], "lo0": [768], "eq": [8], "Wf": [48], "B8": [8], "Zo": [144], "Zw": [144], "Zs": [144],
         "ones": [128], "Id": [12 * 128], "codes": [512], "codeB": [512], "d0": [512], "priO": [256],
         "H": [8, 80], "G": [8, 64], "U": [8, 64], "I": [8, 64], "pri": [8, 64], "py": [8, 16], "e0": [128],
         "rL": [8, 64], "rR": [8, 64], "rT": [8, 64], "NL": [512], "NR": [512], "oh": [2048], "oo": [2048], "opr": [640]},
    F32: {"recF": [8, 32], "recT": [256], "wtf": [8], "nz": [8], "z255": [8], "If": [256], "lk0": [8, 64], "lk1": [8, 64], "lm": [128],
          "kept": [8, 64], "hd": [8, 64], "nd": [8, 64], "hold": [8, 64], "mF": [8, 64], "mH": [256], "dd": [128],
          "c4": [8, 16], "c4u": [8, 16], "c4r": [8, 16], "Cz": [2, 17, 8], "Lz": [8, 17, 8],
          "ol0": [640], "or0": [640], "ol1": [640], "or1": [640], "ot": [128]},
    I32: {"rti": [128], "ui": [128], "uj": [128], "recD": [2, 8, 16], "lr": [768], "own0": [256], "wti": [8],
          "val": [8], "val1": [8], "val4": [8], "pm": [8], "pm2": [8]},
    U16: {"off0": [128], "offc": [128], "offh": [128], "offb": [128], "offu": [128], "offr": [256]},
}
SCRATCH = {k: ("sbuf", [128] + v, d) for d, b in SB.items() for k, v in b.items()}
SCRATCH.update({k: ("psum", [128, 512], F32) for k in ("F0", "F1", "K0", "K1", "L0", "L1")})
SCRATCH.update({k: ("psum", [128, 8, 64], F32) for k in ("L2", "L3")})
DMAS = ["x", "rec", "lr", "rt", "nw", "wt", "t0", "t1", "tf", "tp", "root", "ta", "tb", "tl", "tr", "tm", "o0", "o1", "o2", "o3", "o4", "o5", "o6"]
SEMAPHORES = ["cv", "cs", "cp", "cg", "sent", "arr0", "arr1"] + ["d" + k for k in DMAS]
IO = {"x": [128, 4096], "nw": [128, 2048], "rec": [8, 4096], "lc": [8, 4096], "rc": [8, 4096], "rt": [128, 128], "wt": [128, 1],
      "yl": [8, 20480], "yr": [8, 20480], "yt": [8, 2048]}
SC = [1, -1, 2, -2, 3, -3, 8, -8, -2048, 32768, 8192, -8192]
s_ = np.s_
Op, Fn = AluOpType, ActivationFunctionType
ORDER = []
CY, LAT, GA, PC, EPS, HOLD = 0.00092, 0.12, 1.56, 0.00045, 0.05, 0.6


def plan(g, T, send, n_arr):
    ops = []; fixed = []; fix = [0]

    def A(name, idx=s_[:], off=None):
        return (name, idx if isinstance(idx, tuple) else (idx,), off)

    def ap(a):
        if not isinstance(a, tuple):
            return a
        x = T[a[0]][a[1]]
        return x.indirect(ap(a[2])) if a[2] is not None else x

    def add(e, key, f, wr, rd):
        r = []
        for a in rd:
            if isinstance(a, tuple):
                r.append(a)
                if a[2] is not None:
                    r.append(a[2])
        ops.append((e, key, f, wr, r)); fixed.append(fix[0] > 0)

    def chain(f):
        def h(*a):
            fix[0] += 1; r = f(*a); fix[0] -= 1
            return r
        return h

    V, S, PE = g.vector, g.scalar, g.tensor
    def memset(o, c): add("v", "cv", lambda: V.memset(ap(o), c), [o], [])
    def cp(o, i): add("v", "cv", lambda: V.tensor_copy(ap(o), ap(i)), [o], [i])
    def tt(o, a, b, op): add("v", "cv", lambda: V.tensor_tensor(ap(o), ap(a), ap(b), op), [o], [a, b])
    def ts(o, a, s1, op0, s2=None, op1=None):
        if op1 is None:
            add("v", "cv", lambda: V.tensor_scalar(ap(o), ap(a), ap(s1), None, op0), [o], [a, s1])
        else:
            add("v", "cv", lambda: V.tensor_scalar(ap(o), ap(a), ap(s1), ap(s2), op0, op1), [o], [a, s1, s2])
    def act(o, i, fn=Fn.Copy, bias=None, scale=None):
        kw = {}
        if bias is not None: kw["bias"] = ap(bias) if isinstance(bias, tuple) else float(bias)
        if scale is not None: kw["scale"] = float(scale)
        add("s", "cs", lambda: S.activation(ap(o), ap(i), fn, **kw), [o], [i, bias])
    def mm(o, l, r, start=True, stop=True): add("p", "cp", lambda: PE.matmul(ap(o), ap(l), ap(r), start, stop), [o], [l, r])
    def mms(o_l_r, start=True, stop=True):
        for k, (o, l, r) in enumerate(o_l_r):
            mm(o, l, r, start and k == 0, stop and k == len(o_l_r) - 1)
    def iota(o, pat, base, cm=0):
        if SCRATCH[o[0]][2] == I32:
            add("g", "cg", lambda: g.iota(ap(o), pat, base, cm), [o], [])
        else:
            add("g", "cg", lambda: g.iota(ap(o), pat, base, cm, allow_small_or_imprecise_dtypes=True), [o], [])
    def asel(o, i, pat, op, base, cm): add("g", "cg", lambda: g.affine_select(ap(o), ap(i), pat, op, 0.0, base, cm), [o], [i])
    def dma(grp, o, i, q="y"):
        add(q, "d" + grp, lambda: (g.sync if q == "y" else g.scalar).dma_start(ap(o), ap(i)), [o], [i])
    def Id(k): j = SC.index(k); return A("Id", s_[:, 128 * j:128 * j + 128])
    If, nIf = A("If", s_[:, 0:128]), A("If", s_[:, 128:256])
    def row(q, a, b, t="tab"): return A(t, s_[q::16, a:b])
    def slot(name, s, n=1): return A(name, s_[:, :, 16 * s:16 * (s + n)])
    def half(name, s, ch): return A(name, s_[:, :, 16 * s + 8 * ch:16 * s + 8 * ch + 8])
    def cz(k, name="Cz"): return A(name, s_[:, k, 1::2, :])
    def Fq(ch, q): return A("F%d" % ch, s_[:, 64 * q:64 * q + 64])
    def col(name, a, n): return A(name, s_[:, a:a + n])
    def blk(name, j, n=1): return col(name, 128 * j, 128 * n) if name in ("L0", "L1") else A(name, s_[:, 2 * j:2 * (j + n), :])

    def lh(name, t, s, ch, i8, a=0):
        if t == 0 and s == 0:
            return col(name, a + 1024 * ch + 128 * i8, 128)
        return A(name, s_[:, a + 1024 * ch + i8:a + 1024 * ch + 1024:8])
    def span(ch, h): return (64 * ch, 64) if h is None else (64 * ch + h[0], h[1])
    @chain
    def info(t, s, ch, h=None, by=act):
        off = "off0" if t == 0 and s == 0 else "offc"
        a, n = span(ch, h)
        by(col("gi", 16 * a, 16 * n), A("tab", s_[:, 0:4096 if t == 0 else 14336], col(off, a, n)))
    @chain
    def fwd_info(t, s, ch):
        mms([(A("F%d" % ch, s_[:, i8:384:8]), lh("gi", t, s, ch, i8), A("Wf")) for i8 in range(8)] + [(Fq(ch, 3), Id(-1), half("py", 0, ch))])
    def comp0(src, Z, ch, h=None):
        a, n = span(ch, h)
        o = col("K%d" % ch, 64 + a - 64 * ch, n)
        mms([(o, col(Z, 16 - i, 128), A(src, s_[:, 16 * a + i:16 * (a + n):16])) for i in range(16)])
    comp = chain(comp0)
    @chain
    def cph(ch, h=None, dst="offh"):
        a, n = span(ch, h)
        cp(col(dst, a, n), col("K%d" % ch, 64 + a - 64 * ch, n))
    @chain
    def gat(t, s, ch, h):
        off = "offh" if t else ("off0" if s == 0 else "offc")
        h, n = h if t else (32 * h, 32)
        a = 64 * ch + h
        y = col("y1", 16 * a, 16 * n) if t else (col("X", 4096 + 16 * a, 512) if s == 0 else col("yp", 16 * a, 512))
        tt(col("gx", 16 * a, 16 * n), A("X", s_[:, 0:6144 if t else 4096], col(off, a, n)), y, Op.is_gt)
        if h + n == 64:
            for i8 in range(8):
                mm(A("F%d" % ch, s_[:, 384 + i8:448:8]), lh("gx", t, s, ch, i8), A("B8"))
    @chain
    def back(ch, blocks):
        o = col("K%d" % ch, 0, 64); l = []
        for name, b in blocks:
            l.append((o, A(name, s_[:, b, 1:17, :]), A("If", s_[:, 0:128:2])))
            l.append((o, A(name, s_[:, b, 0:16, :]), A("If", s_[:, 1:128:2])))
        mms(l)
    @chain
    def sel(t, s, ch):
        ts(half("H", s, ch), Fq(ch, 6), 8.5, Op.is_gt)
        if s == 4:
            return
        tt(col("dd", 64 * ch, 64), Fq(ch, 0), half("H", s, ch), Op.mult)
        tt(cz(ch), Fq(ch, 1), col("dd", 64 * ch, 64), Op.add)
        back(ch, [("Cz", ch)])
        tt(half("kept", s, ch), Fq(ch, 2), cz(ch), Op.subtract)
    @chain
    def cpc(ch, dst="offc"): cp(col(dst, 64 * ch, 64), col("K%d" % ch, 0, 64))
    def keep_c(s, ch): act(half("hold", s + 1, ch) if s < 3 else half("c4", 0, ch), cz(ch))
    def keep_p(t, s, ch):
        act(half("G", s, ch), Fq(ch, 3), Fn.Relu, scale=-1)
        if s == 0:
            act(half("hold", 0, ch), Fq(ch, 4))
        if t == 0:
            act(half("pri", s, ch), Fq(ch, 5))
    def side(t, s, ch): keep_c(s, ch); keep_p(t, s, ch)
    def out_hl(ps, n, oc):
        act(col("oh", oc, n), ps); tt(col("oo", oc, n), ps, col("oh", oc, n), Op.subtract)
    def turn(bank, nm, r, start=True, stop=True):
        for j in range(4):
            mm(blk(bank, j), A(nm, s_[:, :, j:64:4]), r, start and j == 0, stop and j == 3)
    def sums(name, t, a):
        for b in range(16):
            mm(A("L1", s_[:, b:128:16]), lh(name, t, 0, b // 8, b % 8, a), A("B8"))
        act(A("py"), blk("L1", 0))

    def st_I(a, n): act(slot("I", a, n), slot("hold", a, n), Fn.Relu, bias=1, scale=-1)
    def st_U():
        mms([(A("L2"), Id(1), A("G"))] + [(slot("L2", k, 4 - k), Id(1), slot("G", 0, 4 - k)) for k in (1, 2, 3)])
        act(A("U"), A("L2"), Fn.Relu, bias=1, scale=-1)
    def st_T():
        l = [(A("L3"), Id(8), A("U")), (A("L3"), Id(-8), A("I"))]
        for s in range(3):
            l += [(slot("L3", s), Id(3 - s), slot("U", s + 1)), (slot("L3", s), Id(s - 3), slot("I", s + 1))]
        mms(l); act(A("rT"), A("L3"), Fn.Relu, bias=-7)
    def st_AB():
        a = [(A("L0"), Id(1), A("codes"))]; b = [(A("L1"), Id(1), A("codeB"))]
        for s in range(4):
            p0, p1 = A("L0", s_[:, 3 - s::4]), A("L1", s_[:, 3 - s::4])
            a += [(p0, Id(-8), slot(k, s)) for k in ("U", "I", "H")[:3 if s < 3 else 2]]
            b += [(p1, Id(-8), slot("U", s)), (p1, Id(8), slot("H", s))][:2 if s < 3 else 1]
        mms(a, True, False); mms(b, True, False)
        for k in range(2):
            mms([(A("L%d" % (2 + k)), Id(-8), A("U")), (slot("L%d" % (2 + k), 0, 3), Id(8 if k else -8), slot("H", 0, 3))], True, False)
    def st_scan():
        for k in range(2):
            mm(A("L%d" % k, s_[:, 0::4]), Id(8 if k else -8), slot("H", 3), False, True)
        for k in range(2):
            nm, bank, r = (("NL", "L0", "rL"), ("NR", "L1", "rR"))[k]
            add("v", "cv", lambda nm=nm, bank=bank: V.tensor_tensor_scan(T[nm][:], T["d0"][:], T[bank][:], 0.0, Op.min, Op.max), [A(nm)], [A("d0"), A(bank)])
            mms([(slot("L%d" % (2 + k), s), Id(1), A(nm, s_[:, 2 - s::4])) for s in range(3)], False, True)
            act(A(r), A("L%d" % (2 + k)), Fn.Relu, bias=-8 if k else 0)
    def st_R():
        mm(A("L1"), nIf, A("kept"), True, False)
        mms([(A("L2"), Id(32768), A(k)) for k in ("rT", "rL", "rR")])
        mms([(A("L1"), Id(-2048), A(k)) for k in ("rT", "rL", "rR")], False, True)
        mm(col("F1", 0, 128), Id(32768), A("NL", s_[:, 3::4])); mm(col("F1", 128, 128), Id(32768), A("NR", s_[:, 3::4]))
        turn("L0", "kept", If, True, False); turn("L3", "kept", If, True, False)
    def st_mF(t):
        tt(A("mF"), A("L2"), A("lk%d" % t), Op.min); tt(slot("mF", 3), slot("mF", 3), A("c4r"), Op.add); tt(A("L1"), A("L1"), A("mF"), Op.add)
    o0, o1 = blk("L2", 0), blk("L2", 1)
    def st_mH(t):
        for k in range(2):
            tt(col("mH", 128 * k, 128), col("F1", 128 * k, 128), slot("lk%d" % t, 0), Op.min)
        mms([(o0, col("mH", 0, 128), If), (o0, A("NL", s_[:, 3::4]), Id(-2048)), (o0, A("c4u"), If),
             (o1, col("mH", 128, 128), If), (o1, A("NR", s_[:, 3::4]), Id(-2048))], True, False)
    def st_c4u(): tt(A("c4u"), A("c4"), slot("U", 3), Op.mult); tt(A("c4r"), A("c4"), A("c4u"), Op.subtract)
    def st_hd():
        tt(A("hd"), A("L1"), slot("H", 0, 4), Op.mult); turn("L0", "hd", If, False, True)
        tt(A("nd"), A("L1"), A("hd"), Op.subtract); turn("L3", "nd", If, False, True)
    outs = []
    def st_n(t, k):
        o = col(("ol%d", "or%d")[k] % t, 0, 512); b = 10240 * t; ps = A(("L0", "L3")[k])
        def out():
            act(o, ps); dma("o%d" % (3 * t + k), A(("yl", "yr")[k], s_[:, b:b + 8192]), o, "ys"[t * k])
        if t:
            return out()
        outs.append(chain(out)); out_hl(ps, 512, 512 * k)
        dma(("tl", "tr")[k], row(2 * k, 4096, 12288), col("oh", 512 * k, 512)); dma(("tl", "tr")[k], row(2 * k + 1, 4096, 12288), col("oo", 512 * k, 512))
    def st_M(t):
        tt(A("c4r"), A("c4u"), slot("H", 4), Op.mult)
        mms([(o0, A("c4r"), nIf), (o1, A("c4r"), If)], False, True)
        def out():
            b = 10240 * t + 8192
            act(col("ol%d" % t, 512, 128), o0); dma("o%d" % (3 * t + 2), A("yl", s_[:, b:b + 2048]), col("ol%d" % t, 512, 128))
            act(col("or%d" % t, 512, 128), o1); dma("o%d" % (3 * t + 2), A("yr", s_[:, b:b + 2048]), col("or%d" % t, 512, 128), "ys"[t])
        if t:
            return out()
        outs.append(chain(out)); out_hl(blk("L2", 0, 2), 256, 1536)
        for k in range(4):
            dma("tm", row(k, 12288, 14336), col(("oh", "oo")[k % 2], 1536 + 128 * (k // 2), 128))
    def st_root(t):
        o = blk("L1", 0)
        mms([(blk("L1", 1), Id(1), slot(k, 0)) for k in ("G", "I")])
        act(A("e0"), blk("L1", 1), Fn.Relu, bias=1, scale=-1)
        mms([(o, A("lm"), If), (o, A("ones"), Id(8192)), (o, A("e0"), Id(-8192))])
        if t:
            act(A("ot"), o, Fn.Relu, bias=10240); dma("o6", A("yt"), A("ot"))
        else:
            out_hl(o, 128, 1792)
            dma("root", row(4, 0, 2048, "xs"), col("oh", 1792, 128)); dma("root", row(5, 0, 2048, "xs"), col("oo", 1792, 128))
    @chain
    def newc(ch, h):
        a = 64 * ch + 32 * h
        tt(col("vv", 16 * a, 512), A("X", s_[:, 0:4096], col("offb", a, 32)), col("yp", 16 * a, 512), Op.add)
    @chain
    def post(ch):
        a = col("vv", 1024 * ch, 1024); b = col("tn", 1024 * ch, 1024)
        ts(b, a, 16.0, Op.is_ge, -16.0, Op.mult)
        add("g", "sent", lambda: send(ap(a), ap(b), T["y1"][:, 1024 * ch:1024 * ch + 1024], "arr%d" % ch), [], [a, b])
        add(None, "arr%d" % ch, None, [col("y1", 1024 * ch, 1024)], [])
    def start(ch):
        comp0("y1", "Zw", ch)
        cp(col("ui", 64 * ch, 64), col("K%d" % ch, 64, 64))
        ts(col("uj", 64 * ch, 64), col("ui", 64 * ch, 64), 2047, Op.bitwise_and)
        cp(col("offu", 64 * ch, 64), col("uj", 64 * ch, 64))
    def roots(ch, by):
        by(col("gi", 1024 * ch, 1024), A("xs", s_[:, 0:2048], col("offu", 64 * ch, 64)))
        comp0("gi", "Zo", ch)
    @chain
    def fetch(s, ch):
        info(1, s, ch, (0, 16)); comp("gi", "Zo", ch, (0, 16)); info(1, s, ch, (16, 48))

    fix[0] = 1
    for z in range(2):
        dma("rec", A("recD", s_[:, z, :, :]), A("rec", s_[z::2, :]), "ys"[z])
    dma("lr", col("lr", 0, 256), A("lc")); dma("lr", col("lr", 256, 256), A("rc"), "s")
    dma("rt", A("rti"), A("rt"))
    dma("x", A("xs"), A("x"), "s")
    dma("nw", col("X", 4096, 2048), A("nw"), "s")
    add("y", "dwt", lambda: g.sync.dma_start(T["wti"][:, 0:1], T["wt"][:]), [col("wti", 0, 1)], [])
    iota(A("val"), [[-16, 8]], 0, 1); iota(A("pm"), [[0, 8]], 0, 1); iota(A("ones"), [[0, 128]], 1)
    asel(Id(1), A("ones"), [[-1, 128]], Op.is_equal, 0, 1)
    iota(col("tab", 2560, 1536), [[0, 1536]], 0); iota(A("own0"), [[1, 256]], 0, 256)
    memset(col("tab", 0, 2560), 0.0); memset(A("Zs"), 0.0)
    ts(A("pm2"), A("pm"), 15, Op.bitwise_and)
    ts(A("val1"), A("val"), 1, Op.arith_shift_right); ts(A("val4"), A("val"), 4, Op.arith_shift_right)
    ts(A("nz"), A("pm2"), 0.0, Op.is_gt); ts(A("z255"), A("pm2"), 0.0, Op.is_equal, 255.0, Op.mult)
    ts(A("B8"), A("val4"), 0.0, Op.is_equal); ts(A("Zs", s_[:, 16::16]), A("val4"), 0.0, Op.is_equal)
    for z in range(2):
        cp(A("recF", s_[:, :, 16 * z:16 * z + 16]), A("recD", s_[:, z, :, :]))
    add("v", "cv", lambda: V.transpose(T["recT"][:], T["recF"][:]), [A("recT")], [A("recF")])
    for b in range(8):
        cp(A("offr", s_[:, b::8]), col("recT", 32 * b, 32))
    ts(A("lr", s_[:, 0:512:256]), A("lr", s_[:, 0:512:256]), col("nz", 0, 1), Op.mult)
    cp(col("hi0", 0, 512), col("lr", 0, 512))
    tt(col("lo0", 0, 512), col("lr", 0, 512), col("hi0", 0, 512), Op.subtract)
    for k in range(2):
        dma("t0", row(2 * k, 0, 4096), col("hi0", 256 * k, 256)); dma("t0", row(2 * k + 1, 0, 4096), col("lo0", 256 * k, 256))
    fix[0] = 0
    act(If, Id(1)); act(nIf, Id(1), scale=-1)
    for k in SC[1:]:
        act(Id(k), Id(1), scale=k)
    iota(A("Cz"), [[0, 272]], 0); iota(A("lm"), [[0, 8], [128, 16]], 4096, 1)
    for b in range(16):
        asel(A("yp", s_[:, 1024 * (b // 8) + b % 8:1024 * (b // 8) + 1024:8]), col("X", 4096 + 128 * b, 128), [[0, 128]], Op.is_ge, 0, 0)
    iota(A("Lz", s_[:, :, 0::2, :]), [[0, 576]], 0)
    iota(A("codes"), [[0, 128], [1, 4]], 2); iota(A("codeB"), [[0, 128], [1, 4]], -6)
    iota(A("d0"), [[0, 128], [8, 4]], 0); iota(A("lk0"), [[0, 8], [0, 4], [128, 16]], 4096 + 10240, 1)
    iota(A("lk1"), [[0, 8], [0, 4], [128, 16]], 4096 + 20480, 1)

    pr = []; fix[0] = 1
    for k in range(4):
        for e in range(2):
            a = 2048 * e + 512 * k
            (cp, act)[e](col("X", a, 512), A("xs", s_[:, :], col("offr", a // 16, 32)))
            if a == 0:
                memset(col("X", 0, 1), 0.0)
            for x in (a // 256, a // 256 + 1):
                mm(blk("L0", 0, 2), col("Zs", 16 - x, 128), col("X", 256 * x, 256), not pr, len(pr) == 15); pr.append(x)
    act(A("priO"), blk("L0", 0, 2)); act(col("priO", 0, 1), col("L0", 0, 1), Fn.Relu, bias=col("z255", 0, 1))
    dma("tp", row(6, 0, 4096), A("priO"), "s")
    cp(A("off0"), A("rti")); fix[0] = 0; gat(0, 0, 0, 0)
    ts(col("lr", 512, 256), A("own0"), 4095, Op.bitwise_and); cp(col("hi0", 512, 256), col("lr", 512, 256))
    tt(col("lo0", 512, 256), col("lr", 512, 256), col("hi0", 512, 256), Op.subtract)
    dma("t1", row(4, 0, 4096), col("hi0", 512, 256)); dma("t1", row(5, 0, 4096), col("lo0", 512, 256))
    sums("X", 0, 4096)
    mm(blk("L0", 0), A("lm"), If); mm(blk("L0", 1), A("py"), Id(1))
    out_hl(blk("L0", 0), 128, 1920); act(col("opr", 512, 128), blk("L0", 1))
    for a, n in ((4096, 4096), (8192, 4096), (12288, 2048)):
        add("y", "dtf", lambda a=a, n=n: g.sync.dma_start(T["tab"][:, a:a + n], T["x"][:, 0:n]), [col("tab", a, n)], [row(6, 0, 16)])
    dma("ta", row(4, 12288, 14336), col("oh", 1920, 128)); dma("ta", row(5, 12288, 14336), col("oo", 1920, 128)); dma("ta", row(6, 12288, 14336), col("opr", 512, 128))
    ts(col("Wf", 8, 8), A("val1"), 1.0, Op.is_equal); ts(A("eq"), A("val1"), 0.0, Op.is_equal)
    ts(col("Wf", 24, 8), A("val"), 6.0, Op.is_equal); ts(col("Wf", 32, 8), A("val1"), 2.0, Op.is_equal)
    ts(col("Wf", 40, 8), A("val"), 6.0, Op.is_equal)
    tt(col("Wf", 0, 8), A("eq"), col("Wf", 8, 8), Op.subtract); tt(col("Wf", 16, 8), A("eq"), col("Wf", 8, 8), Op.add)
    gat(0, 0, 0, 1); gat(0, 0, 1, 0); gat(0, 0, 1, 1)
    memset(A("Zo"), 0.0); memset(A("Zw"), 0.0); cp(col("wtf", 0, 1), col("wti", 0, 1))
    cp(A("Zo", s_[:, 16::16]), col("Wf", 32, 8)); ts(A("Zw", s_[:, 16::16]), A("B8"), col("wtf", 0, 1), Op.mult)
    info(0, 0, 0); info(0, 0, 1, None, cp)
    fwd_info(0, 0, 0); fwd_info(0, 0, 1)
    sel(0, 0, 0); sel(0, 0, 1); cpc(0)
    for s in range(1, 4):
        info(0, s, 0); side(0, s - 1, 0)
        gat(0, s, 0, 0)
        if s > 1:
            sel(0, s - 1, 1); fwd_info(0, s, 0); gat(0, s, 0, 1); cpc(1)
        else:
            cpc(1); fwd_info(0, s, 0); gat(0, s, 0, 1)
        info(0, s, 1); side(0, s - 1, 1)
        if s == 1:
            st_I(0, 1); st_root(0)
        if s == 3:
            st_I(1, 3); act(cz(7, "Lz"), half("hold", 3, 1)); act(cz(3, "Lz"), half("hold", 3, 0))
            turn("L0", "hold", If); out_hl(A("L0"), 512, 1024)
        gat(0, s, 1, 0)
        if s == 3:
            for k in range(3):
                tt(cz(4 + k, "Lz"), half("hold", k, 1), half("I", k + 1, 1), Op.mult)
        sel(0, s, 0)
        if s == 3:
            back(1, [("Lz", 4 + k) for k in range(4)])
        fwd_info(0, s, 1)
        gat(0, s, 1, 1); cpc(0)
    cpc(1, "offb")
    for k in range(3):
        tt(cz(k, "Lz"), half("hold", k, 0), half("I", k + 1, 0), Op.mult)
    back(0, [("Lz", k) for k in range(4)])
    keep_p(0, 3, 0); keep_p(0, 3, 1); keep_c(3, 0)
    st_U(); st_T()
    turn("L1", "pri", Id(1)); act(col("opr", 0, 512), A("L1"))
    dma("tb", row(4, 4096, 12288), col("oh", 1024, 512)); dma("tb", row(5, 4096, 12288), col("oo", 1024, 512)); dma("tb", row(6, 4096, 12288), col("opr", 0, 512))
    newc(1, 0); sel(0, 3, 1); cpc(0, "offb"); keep_c(3, 1)
    newc(1, 1); cpc(1); post(1)
    st_AB()
    newc(0, 0); st_c4u(); st_scan(); st_R()
    newc(0, 1); post(0)
    st_mF(0); st_hd(); st_n(0, 0); st_n(0, 1); st_mH(0)
    gat(0, 4, 0, 0); gat(0, 4, 0, 1); gat(0, 4, 1, 0); sel(0, 4, 0); gat(0, 4, 1, 1); sel(0, 4, 1)
    st_M(0); start(1); roots(1, cp); start(0); roots(0, act); sums("y1", 1, 0)

    cph(1, None, "offc"); cph(0, None, "offc"); fetch(0, 0)
    prev = None
    for s in range(5):
        for ch in range(2):
            cph(ch, (0, 16)); gat(1, s, ch, (0, 16))
            comp("gi", "Zo", ch, (16, 48))
            if prev:
                sel(1, *prev)
            else:
                fetch(0, 1)
            if s < 4:
                fwd_info(1, s, ch); keep_p(1, s, ch)
            if (s, ch) == (3, 1):
                st_I(2, 2); st_U(); st_T(); st_AB()
            if (s, ch) == (4, 1):
                st_hd(); st_n(1, 0); st_n(1, 1)
            cph(ch, (16, 48)); gat(1, s, ch, (16, 8))
            if prev and prev[0] < 4:
                cpc(prev[1]); fetch(prev[0] + 1, prev[1]); keep_c(*prev)
            if (s, ch) == (4, 0):
                st_c4u(); st_scan(); st_R()
            gat(1, s, ch, (24, 40))
            if s == 0 or (s, ch) == (1, 0):
                outs[2 * s + ch]()
            if (s, ch) == (1, 1):
                st_I(0, 2); st_root(1)
            if (s, ch) == (4, 0):
                st_mF(1); st_mH(1)
            prev = (s, ch)
    sel(1, 4, 1); st_M(1)

    total = {}
    for e, key, f, wr, rd in ops:
        total[key] = total.get(key, 0) + (1 if key[0] == "c" else 16 if key[0] == "d" else n_arr[key])
    if not ORDER:
        ORDER.extend(arrange(ops, fixed))
    order, deps = ORDER
    Q = {"v": V, "s": S, "p": PE, "g": g, "y": g.sync}
    cnt = {}; val = {}; seen = {q: {} for q in Q}
    for n in order:
        e, key, f, wr, rd = ops[n]
        cnt[key] = cnt.get(key, 0) + 1
        val[n] = cnt[key] if key[0] == "c" else total[key]
        if e is None:
            continue
        need = {}
        for m in deps[n]:
            k = ops[m][1]
            need[k] = max(need.get(k, 0), val[m])
        for k, v in sorted(need.items()):
            if seen[e].get(k, 0) < v:
                Q[e].wait_ge(T.sem[k], int(v)); seen[e][k] = v
        ins = f()
        if key != "sent":
            ins.then_inc(T.sem[key], 1 if key[0] == "c" else 16)
    for k, v in sorted(total.items()):
        if max(seen[q].get(k, 0) for q in Q) < v:
            g.wait_ge(T.sem[k], int(v))


def arrange(ops, fixed):
    shapes = dict(IO); shapes.update({k: v[1] for k, v in SCRATCH.items()})
    els = {k: np.arange(int(np.prod(v[1:]))).reshape(v[1:]) for k, v in shapes.items()}
    rows = ("tab", "xs")

    def bits(a):
        ix = els[a[0]][a[1][1:]].ravel(); n = els[a[0]].size
        if a[0] in rows:
            ix = (np.unique(np.arange(128)[a[1][0]] % 16)[:, None] * n + ix).ravel(); n *= 16
        m = np.zeros(n, np.uint8); m[ix] = 1
        return int.from_bytes(np.packbits(m).tobytes(), "big")

    def kind(a): return SCRATCH[a[0]] if a[0] in SCRATCH else ("dram", 0, F32)
    N = len(ops); group = {}
    for n, o in enumerate(ops):
        group.setdefault(o[1], []).append(n)
    deps = []; after = []; cost = []; log = {}; bank = {}; first = {}
    for n, (e, key, f, wr, rd) in enumerate(ops):
        d = set(); a2 = set()
        for a, w in [(a, False) for a in rd] + [(a, True) for a in wr]:
            if kind(a)[0] == "psum":
                b = bank.setdefault(a[0], {})
                d.update(m for k, m in b.items() if k != key); a2.update(m for k, m in b.items() if k == key)
                b[key] = n
                if key == "cp":
                    continue
            x = bits(a); l = log.setdefault(a[0], [])
            d.update(m for m, y, w2 in l if (w or w2) and x & y)
            if w:
                l[:] = [t for t in l if t[1] & ~x]
            l.append((n, x, w))
        d = set(m for m in d if m != n and not (ops[m][1] == key and key[0] == "d"))
        for m in list(d):
            if ops[m][1][0] == "d":
                d.update(group[ops[m][1]])
        if fixed[n]:
            a2.add(first.get(e, n)); first[e] = n
        if e is None:
            a2.add(n - 1)
        deps.append(d); after.append(a2 - {n})
        ne = els[wr[0][0]][wr[0][1][1:]].size if wr else 0
        full = [a for a in rd if els[a[0]][a[1][1:]].size > 1]
        if key[0] == "d":
            c = (0.1, 0.3 + ne * (128 if wr[0][1][0] == s_[:] and wr[0][0] in SCRATCH else 8) * (2 if kind(wr[0])[2] == BF else 4) / 3e5)
        elif key[0] != "c":
            c = (0.1, 5.5 if e is None else 0.1)
        elif e == "p":
            c = max(64, ne) * (4 if kind(rd[0])[2] == F32 else 1) * PC
        elif any(a[2] is not None for a in rd):
            c = 0.07 + ne * GA * CY
        elif e == "g" or (e == "v" and len(full) == 2 and all(kind(a)[0] == "sbuf" for a in full)):
            c = 0.1 + 2 * ne * CY
        else:
            c = 0.08 + max(64, ne * (0.5 if e == "v" and all(kind(a)[2] == BF for a in full + wr) else 1)) * CY
        cost.append(c if isinstance(c, tuple) else (c, c))
    succ = [[] for _n in range(N)]
    for n in range(N):
        for m in deps[n] | after[n]:
            assert m < n
            succ[m].append(n)
    rank = [0.0] * N
    for n in reversed(range(N)):
        rank[n] = cost[n][1] + (2.0 if ops[n][1][0] == "d" else 0) + max([rank[k] + (LAT if n in deps[k] else 0) for k in succ[n]], default=0.0)
    left = [len(deps[n] | after[n]) for n in range(N)]; at = [0.0] * N
    ready = [n for n in range(N) if not left[n]]; free = {}; order = []
    while ready:
        t0 = min(max(at[n], free.get(ops[n][0], 0.0)) for n in ready)
        n = max((n for n in ready if max(at[n], free.get(ops[n][0], 0.0)) <= t0 + EPS), key=lambda n: (rank[n], -n))
        e = ops[n][0]; soon = [k for k in ready if ops[k][0] == e and rank[k] > rank[n] and at[k] <= t0 + HOLD * cost[n][0]]
        if soon:
            n = min(soon, key=lambda k: at[k])
        ready.remove(n); order.append(n)
        t = max(at[n], free.get(e, 0.0)); free[e] = t + (cost[n][0] if e else 0)
        end = t + cost[n][1]
        if ops[n][1][0] == "d":
            free["d"] = max(t + 1.2, free.get("d", 0.0)) + cost[n][1]; end = free["d"] + 0.8
        for k in succ[n]:
            at[k] = max(at[k], end + LAT if n in deps[k] or ops[k][0] is None else t)
            left[k] -= 1
            if not left[k]:
                ready.append(k)
    return [order, deps]


def rank_program(g, core, T, topo):
    rank = T.rank_of(core)
    if rank is None:
        return
    n = len(T.cores)
    dst, src = T.cores[(rank + 1) % n], T.cores[(rank - 1) % n]
    rid, pid = topo.addr(dst)[:2]

    def send(a, b, out, sem):
        g.remote_dma_fused([RemoteDMATransfer(dst_ids=[DstId(rid=rid, pnc=pid)], dma_engine_mask=topo.mask(core, dst), remote_sem=T.sem[sem],
                                              srcs=[a, b], dsts=[out], alu_op=1)], local_sem=T.sem["sent"])
    k = len(topo.engines(src, core))
    plan(g, T, send, {"sent": len(topo.engines(core, dst)), "arr0": k, "arr1": k})
